import numpy as np
import ml_dtypes


def mxq(x, axis, fmt="e4m3"):
    dtype, down = {"e4m3": (ml_dtypes.float8_e4m3fn, 7), "e5m2": (ml_dtypes.float8_e5m2, 14)}[fmt]
    v = np.moveaxis(np.asarray(x, np.float32).astype(ml_dtypes.bfloat16).astype(np.float64), axis, -1)
    blocks = v.reshape(v.shape[:-1] + (-1, 32))
    amax = np.abs(blocks).max(-1, keepdims=True)
    byte = np.maximum(np.where(amax > 0, np.frexp(amax)[1] - 1 + 127, 0) - down, 1)
    scale = np.exp2(byte - 127.0)
    codes = (blocks / scale).astype(np.float32).astype(dtype).astype(np.float64)
    return np.moveaxis((codes * scale).reshape(v.shape), -1, axis)


WIDE = False


def mx_kscale(k):
    if not WIDE:
        return np.ones(k)
    levels = np.array([10, -10, 5, -5, 0])
    if k % 512:
        return np.exp2(np.random.permutation(np.resize(levels, k // 32))).repeat(32)
    a = np.empty((k // 512, 16))
    for p in range(k // 512):
        a[p, :8] = np.random.permutation(np.resize(levels, 8))
        for g in range(8):
            far = levels[np.abs(levels - a[p, g]) >= 10]
            a[p, g + 8] = far[np.random.randint(len(far))]
    return np.exp2(a.ravel()).repeat(32)


def f64(x):
    return np.asarray(x).astype(np.float64)


def striped8(idx):
    return np.concatenate([v.reshape(-1, 16).T for v in idx]).astype(np.uint16)


def unstriped8(offs):
    return np.stack([offs[16 * g:16 * g + 16].T.reshape(-1) for g in range(8)]).astype(np.int64)


E2M1 = np.array([0.0, 0.5, 1.0, 1.5, 2.0, 3.0, 4.0, 6.0, -0.0, -0.5, -1.0, -1.5, -2.0, -3.0, -4.0, -6.0])


def pack_weight(w, fmt):
    k, n = w.shape
    w = f64(np.asarray(w, np.float32).astype(ml_dtypes.bfloat16)).reshape(k // 32, 32, n)
    amax = np.abs(w).max(1)
    if fmt == "e4m3":
        byte = np.frexp(amax)[1] - 1 + 127 - 7
    else:
        mant, ex = np.frexp(amax / 6.0)
        byte = np.where(mant > 0.5, ex, ex - 1) + 127
    byte = np.clip(np.where(amax > 0, byte, 1), 1, 254)
    scaled = (w * np.exp2(127.0 - byte)[:, None, :]).reshape(k, n).astype(np.float32)
    by_word = np.ascontiguousarray(scaled.reshape(k // 512, 128, 4, n).transpose(0, 1, 3, 2))
    if fmt == "e4m3":
        words = by_word.astype(ml_dtypes.float8_e4m3fn).view(np.uint8)
    else:
        c = by_word.astype(ml_dtypes.float4_e2m1fn).view(np.uint8) & 0xF
        words = (c[..., 0::2] | (c[..., 1::2] << 4)).reshape(k // 512, 128, 2 * n)
    return np.ascontiguousarray(words), np.ascontiguousarray(byte.astype(np.uint8).reshape(k // 512, 16, n))


def unpack_weight(words, scales, fmt):
    g, _, n = scales.shape
    words = np.ascontiguousarray(words).reshape(g, 128, n, -1)
    if fmt == "e4m3":
        vals = words.view(ml_dtypes.float8_e4m3fn).astype(np.float64)
    else:
        nib = np.empty((g, 128, n, 4), np.uint8)
        nib[..., 0::2] = words & 0xF
        nib[..., 1::2] = words >> 4
        vals = E2M1[nib]
    vals = vals * np.repeat(np.exp2(scales.astype(np.float64) - 127.0), 8, axis=1)[..., None]
    return vals.transpose(0, 1, 3, 2).reshape(g * 512, n)


def gelu(v):
    return 0.5 * v * (1.0 + np.tanh(np.sqrt(2.0 / np.pi) * (v + 0.044715 * v**3)))


K, M, T, S = 1536, 1024, 1024, 512


def setup_inputs():
    n = np.random.standard_normal
    s = mx_kscale(K)[:, None]
    p_w = pack_weight(n((K, M)) / np.sqrt(K) / s, "e4m3")
    return {
        "xT": (n((K, T)) * s).astype(np.float32),
        "w_words": p_w[0],
        "w_scales": p_w[1],
        "wgt": np.repeat(np.random.uniform(0.5, 2.0, (8, S)), 16, axis=0).astype(np.float32),
        "b": (0.3 * n(1024)).astype(np.float32),
        "wgo": np.repeat(np.random.uniform(0.5, 2.0, (8, S)), 16, axis=0).astype(np.float32),
        "offs": striped8(np.stack([np.random.permutation(T)[:S] for _ in range(8)])),
        "offs2": striped8(np.stack([np.random.permutation(T)[:S] for _ in range(8)])),
    }


def reference(xT, w_words, w_scales, wgt, b, wgo, offs, offs2):
    idx = unstriped8(offs)
    group = np.arange(K) % 512 // 64
    xg = f64(wgt)[np.arange(K) // 4 % 128] * f64(xT)[np.arange(K)[:, None], idx[group]]
    xT_ = mxq(xg, 0, "e4m3")
    w_ = unpack_weight(w_words, w_scales, "e4m3")
    y = w_.T @ xT_
    place = unstriped8(offs2)[np.arange(M) % 128 // 16]
    out = np.zeros((M, T))
    out[np.arange(M)[:, None], place] = f64(wgo)[np.arange(M) % 128] * (gelu(y + f64(b)[:, None]))
    return out

@@ -1,0 +1,195 @@
+from contextlib import ExitStack
+
+import concourse.mybir as mybir
+
+F32 = mybir.dt.float32
+BF16 = mybir.dt.bfloat16
+I32 = mybir.dt.int32
+U32 = mybir.dt.uint32
+U16 = mybir.dt.uint16
+U8 = mybir.dt.uint8
+FP8X4 = mybir.dt.float8_e4m3fn_x4
+MULT = mybir.AluOpType.mult
+GELU = mybir.ActivationFunctionType.Gelu_apprx_tanh
+
+K, M, T, S = 1536, 1024, 1024, 512
+P = 128
+PACK = 4
+PASSES = K // (P * PACK)
+ROW_TILES = M // P
+WINDOWS = 4
+HALF = S // 2
+OFF_COLS = HALF // 16
+
+FLOPS = 2 * K * M * S
+
+
+def tile_list_hboth_gelu_kernel(tc, xT, w_words, w_scales, wgt, b, wgo, offs, offs2, out):
+    nc = tc.nc
+    with ExitStack() as ctx:
+        keep = ctx.enter_context(tc.tile_pool(name="keep", bufs=1))
+        psum = ctx.enter_context(tc.psum_pool(name="psum", bufs=8))
+
+        offs_sb = keep.tile([P, S // 16], U16, name="offs_sb")
+        offs2_sb = keep.tile([P, S // 16], U16, name="offs2_sb")
+        wgt_sb = [keep.tile([P, HALF], F32, name=f"wgt{h}") for h in range(2)]
+        wgo_sb = [keep.tile([P, HALF], F32, name=f"wgo{h}") for h in range(2)]
+        x_sb = [[keep.tile([P, T], F32, name=f"x{a}_{i}") for i in range(PACK)] for a in range(PASSES)]
+        w_sb = [[keep.tile([P, M // 2], U32, align_bytes=64, name=f"w{a}_{part}") for part in range(2)] for a in range(PASSES)]
+        w_scale = keep.tile([P, M], U8, align_bytes=64, name="w_scale")
+        b_rows = keep.tile([P, 32], F32, align_bytes=64, name="b_rows")
+        b_col = keep.tile([P, 32], F32, align_bytes=64, name="b_col")
+        warm = keep.tile([P, 1], F32, name="warm")
+        windows = [keep.tile([P, T], F32, name=f"window{r}") for r in range(WINDOWS)]
+        picked = [[keep.tile([P, PACK, HALF], F32, name=f"picked{a}_{h}") for h in range(2)] for a in range(PASSES)]
+        grouped = [keep.tile([P, S, PACK], BF16, align_bytes=64, name=f"grouped{a}") for a in range(PASSES)]
+        codes = [keep.tile([P, S], U32, align_bytes=64, name=f"codes{a}") for a in range(PASSES)]
+        scales = [keep.tile([P, S], U8, align_bytes=64, name=f"scales{a}") for a in range(PASSES)]
+        acted = [keep.tile([P, S], F32, name=f"acted{r}") for r in range(ROW_TILES)]
+
+        def load_x(a, i):
+            rows = xT.rearrange("(a p i) t -> a i p t", a=PASSES, i=PACK)
+            nc.sync.dma_start(x_sb[a][i][:], rows[a, i])
+
+        def load_wgo(h):
+            nc.sync.dma_start(wgo_sb[h][:], wgo[:, h * HALF : (h + 1) * HALF])
+
+        nc.vector.memset(warm[:], 0.0)
+        nc.vector.memset(b_rows[:], 0.0)
+        nc.vector.memset(w_scale[:].bitcast(I32), 0)
+        for i, window in enumerate(windows):
+            engine = nc.vector if i < 2 else nc.gpsimd
+            engine.memset(window[:].bitcast(I32), 0)
+        b_view = b.rearrange("(r q i) -> q r i", q=4, i=32)
+        for q in range(4):
+            nc.scalar.dma_start(b_rows[32 * q : 32 * q + ROW_TILES, :], b_view[q])
+        nc.scalar.activation(warm[:], warm[:], GELU)
+
+        nc.sync.dma_start(offs_sb[:], offs)
+        nc.sync.dma_start(wgt_sb[0][:], wgt[:, 0:HALF])
+        load_x(0, 0)
+        nc.sync.dma_start(wgt_sb[1][:], wgt[:, HALF:S])
+        for i in range(1, PACK):
+            load_x(0, i)
+        for i in range(PACK):
+            load_x(1, i)
+        load_x(2, 0)
+        nc.sync.dma_start(offs2_sb[:], offs2)
+        load_wgo(0)
+        for i in range(1, PACK):
+            load_x(2, i)
+        for q in range(4):
+            nc.sync.dma_start(
+                w_scale[32 * q : 32 * q + 4 * PASSES, :].bitcast(I32),
+                w_scales[:, 4 * q : 4 * q + 4, :].bitcast(I32),
+            )
+        for part in range(2):
+            cols = slice(part * M // 2, (part + 1) * M // 2)
+            for a in range(PASSES):
+                nc.sync.dma_start(
+                    w_sb[a][part][:].bitcast(I32),
+                    w_words[a, :, cols, :].rearrange("p n i -> p (n i)").bitcast(I32),
+                )
+        load_wgo(1)
+
+        def gather(a, i, h):
+            nc.vector.tensor_tensor(
+                picked[a][h][:, i, :],
+                x_sb[a][i][:].indirect(offs_sb[:, h * OFF_COLS : (h + 1) * OFF_COLS]),
+                wgt_sb[h][:],
+                MULT,
+            )
+
+        def interleave(a, h):
+            nc.scalar.copy(
+                out=grouped[a][:, h * HALF : (h + 1) * HALF, :].rearrange("p (c i) t -> p c t i", i=4),
+                in_=picked[a][h][:].rearrange("p t (c i) -> p c t i", i=4),
+            )
+
+        def quantize(a, first, last):
+            nc.vector.quantize_mx(
+                out=codes[a][:, first:last].bitcast(FP8X4),
+                scales=scales[a][:, first:last],
+                in_=grouped[a][:, first:last, :].rearrange("p c t -> p (c t)"),
+            )
+
+        def project(r, first, last):
+            acc = psum.tile([P, S], F32, name="acc")
+            cols = slice(r * P, (r + 1) * P)
+            part, w_first = divmod(r * P, M // 2)
+            for a in range(PASSES):
+                nc.tensor.matmul_mx(
+                    out=acc[:, first:last],
+                    lhsT=w_sb[a][part][:, w_first : w_first + P].bitcast(FP8X4),
+                    lhsT_scale=w_scale[4 * a :, cols],
+                    rhs=codes[a][:, first:last].bitcast(FP8X4),
+                    rhs_scale=scales[a][:, first:last],
+                    start=(a == 0),
+                    stop=(a == PASSES - 1),
+                )
+            nc.scalar.activation(acted[r][:, first:last], acc[:, first:last], GELU, bias=b_col[:, r : r + 1])
+
+        def scatter(r, h):
+            nc.vector.tensor_tensor(
+                windows[r % WINDOWS][:].indirect(offs2_sb[:, h * OFF_COLS : (h + 1) * OFF_COLS]),
+                acted[r][:, h * HALF : (h + 1) * HALF],
+                wgo_sb[h][:],
+                MULT,
+            )
+
+        def store(r):
+            nc.sync.dma_start(out[r * P : (r + 1) * P, :], windows[r % WINDOWS][:])
+
+        for i in range(PACK):
+            gather(0, i, 0)
+            gather(0, i, 1)
+        interleave(0, 0)
+        interleave(0, 1)
+        for i in range(PACK):
+            gather(1, i, 0)
+        interleave(1, 0)
+        quantize(0, 0, S)
+        for i in range(PACK):
+            gather(1, i, 1)
+        interleave(1, 1)
+        nc.vector.transpose(b_col[:], b_rows[:])
+        for i in range(PACK):
+            gather(2, i, 0)
+        interleave(2, 0)
+        quantize(1, 0, S)
+        gather(2, 0, 1)
+        gather(2, 1, 1)
+        quantize(2, 0, HALF)
+        project(0, 0, HALF)
+        project(1, 0, HALF)
+        gather(2, 2, 1)
+        gather(2, 3, 1)
+        interleave(2, 1)
+        scatter(0, 0)
+        project(2, 0, HALF)
+        project(3, 0, HALF)
+        scatter(1, 0)
+        quantize(2, HALF, S)
+        project(0, HALF, S)
+        project(1, HALF, S)
+        scatter(2, 0)
+        scatter(3, 0)
+        scatter(0, 1)
+        store(0)
+        scatter(1, 1)
+        store(1)
+        project(2, HALF, S)
+        project(3, HALF, S)
+        scatter(2, 1)
+        store(2)
+        scatter(3, 1)
+        store(3)
+        for r in range(4, ROW_TILES, 2):
+            project(r, 0, S)
+            project(r + 1, 0, S)
+            scatter(r, 0)
+            scatter(r + 1, 0)
+            scatter(r, 1)
+            store(r)
+            scatter(r + 1, 1)
+            store(r + 1)

@@ -1,6 +1,7 @@
 from contextlib import ExitStack
 
 import concourse.mybir as mybir
+from concourse.masks import make_identity
 
 F32 = mybir.dt.float32
 BF16 = mybir.dt.bfloat16
@@ -16,10 +17,13 @@ K, M, T, S = 1536, 1024, 1024, 512
 P = 128
 PACK = 4
 PASSES = K // (P * PACK)
+LAST = PASSES - 1
 ROW_TILES = M // P
-WINDOWS = 4
+WINDOWS = 3
 HALF = S // 2
 OFF_COLS = HALF // 16
+EARLY = 2
+W_EARLY = EARLY * P
 
 FLOPS = 2 * K * M * S
 
@@ -28,168 +32,161 @@ def tile_list_hboth_gelu_kernel(tc, xT, w_words, w_scales, wgt, b, wgo, offs, of
     nc = tc.nc
     with ExitStack() as ctx:
         keep = ctx.enter_context(tc.tile_pool(name="keep", bufs=1))
-        psum = ctx.enter_context(tc.psum_pool(name="psum", bufs=8))
+        psum = ctx.enter_context(tc.psum_pool(name="psum", bufs=7))
+        psum_b = ctx.enter_context(tc.psum_pool(name="psum_b", bufs=1))
 
         offs_sb = keep.tile([P, S // 16], U16, name="offs_sb")
         offs2_sb = keep.tile([P, S // 16], U16, name="offs2_sb")
-        wgt_sb = [keep.tile([P, HALF], F32, name=f"wgt{h}") for h in range(2)]
-        wgo_sb = [keep.tile([P, HALF], F32, name=f"wgo{h}") for h in range(2)]
-        x_sb = [[keep.tile([P, T], F32, name=f"x{a}_{i}") for i in range(PACK)] for a in range(PASSES)]
-        w_sb = [[keep.tile([P, M // 2], U32, align_bytes=64, name=f"w{a}_{part}") for part in range(2)] for a in range(PASSES)]
+        slots = keep.tile([P, 8, HALF], F32, name="slots")
+        wgt_sb = slots[:, 0:2, :].rearrange("p h c -> p (h c)")
+        picked_last = [slots[:, 4:8, :], slots[:, 0:8:2, :]]
+        wgo_sb = keep.tile([P, S], F32, name="wgo_sb")
+        x_sb = [[keep.tile([P, T], F32, align_bytes=64, name=f"x{a}_{i}", tag=f"x{a}_{i}") for i in range(PACK)] for a in range(PASSES)]
+        w_early = keep.tile([P, PASSES, W_EARLY], U32, align_bytes=64, name="w_early")
+        w_late = keep.tile([P, PASSES, M - W_EARLY], U32, align_bytes=64, name="w_late")
         w_scale = keep.tile([P, M], U8, align_bytes=64, name="w_scale")
-        b_rows = keep.tile([P, 32], F32, align_bytes=64, name="b_rows")
-        b_col = keep.tile([P, 32], F32, align_bytes=64, name="b_col")
+        ident = keep.tile([P, P], F32, name="ident")
+        b_rows = keep.tile([P, P], F32, name="b_rows")
+        b_col = keep.tile([P, ROW_TILES], F32, name="b_col")
         warm = keep.tile([P, 1], F32, name="warm")
         windows = [keep.tile([P, T], F32, name=f"window{r}") for r in range(WINDOWS)]
-        picked = [[keep.tile([P, PACK, HALF], F32, name=f"picked{a}_{h}") for h in range(2)] for a in range(PASSES)]
-        grouped = [keep.tile([P, S, PACK], BF16, align_bytes=64, name=f"grouped{a}") for a in range(PASSES)]
-        codes = [keep.tile([P, S], U32, align_bytes=64, name=f"codes{a}") for a in range(PASSES)]
+        picked = [keep.tile([P, PACK, S], F32, name=f"picked{a}") for a in range(LAST)]
+        grouped = [keep.tile([P, S * PACK], BF16, align_bytes=64, name=f"grouped{a}") for a in range(LAST)]
+        b_first = keep.tile([P, 1], F32, align_bytes=64, name="b_first", tag="grouped2_1")
+        grouped2 = [keep.tile([P, HALF * PACK], BF16, align_bytes=64, name=f"grouped2_{h}", tag=f"grouped2_{h}") for h in range(2)]
+        codes = [
+            keep.tile([P, S], U32, align_bytes=64, name="codes0"),
+            keep.tile([P, S], U32, align_bytes=64, name="codes1", tag="x2_0"),
+            keep.tile([P, S], U32, align_bytes=64, name="codes2"),
+        ]
         scales = [keep.tile([P, S], U8, align_bytes=64, name=f"scales{a}") for a in range(PASSES)]
         acted = [keep.tile([P, S], F32, name=f"acted{r}") for r in range(ROW_TILES)]
+
+        def acted_cols(r, first, last):
+            if (r, first) == (1, 0):
+                return slots[:, 2, :]
+            return acted[r][:, first:last]
 
         def load_x(a, i):
             rows = xT.rearrange("(a p i) t -> a i p t", a=PASSES, i=PACK)
             nc.sync.dma_start(x_sb[a][i][:], rows[a, i])
 
-        def load_wgo(h):
-            nc.sync.dma_start(wgo_sb[h][:], wgo[:, h * HALF : (h + 1) * HALF])
+        def load_w(tile, first, last):
+            nc.sync.dma_start(
+                tile[:].bitcast(I32),
+                w_words[:, :, first:last, :].rearrange("a p n i -> p a (n i)").bitcast(I32),
+            )
 
         nc.vector.memset(warm[:], 0.0)
+        nc.scalar.activation(warm[:], warm[:], GELU)
         nc.vector.memset(b_rows[:], 0.0)
         nc.vector.memset(w_scale[:].bitcast(I32), 0)
-        for i, window in enumerate(windows):
-            engine = nc.vector if i < 2 else nc.gpsimd
-            engine.memset(window[:].bitcast(I32), 0)
-        b_view = b.rearrange("(r q i) -> q r i", q=4, i=32)
-        for q in range(4):
-            nc.scalar.dma_start(b_rows[32 * q : 32 * q + ROW_TILES, :], b_view[q])
-        nc.scalar.activation(warm[:], warm[:], GELU)
+
+        make_identity(nc, ident[:])
+        for window in windows:
+            nc.gpsimd.memset(window[:].bitcast(I32), 0)
 
         nc.sync.dma_start(offs_sb[:], offs)
-        nc.sync.dma_start(wgt_sb[0][:], wgt[:, 0:HALF])
         load_x(0, 0)
-        nc.sync.dma_start(wgt_sb[1][:], wgt[:, HALF:S])
-        for i in range(1, PACK):
-            load_x(0, i)
-        for i in range(PACK):
-            load_x(1, i)
-        load_x(2, 0)
-        nc.sync.dma_start(offs2_sb[:], offs2)
-        load_wgo(0)
-        for i in range(1, PACK):
-            load_x(2, i)
+        nc.sync.dma_start(wgt_sb, wgt)
+        for a in range(PASSES):
+            for i in range(PACK):
+                if (a, i) != (0, 0):
+                    load_x(a, i)
+            if a == 0:
+                nc.sync.dma_start(b_rows[0:ROW_TILES, :], b.rearrange("(r p) -> r p", p=P))
         for q in range(4):
             nc.sync.dma_start(
                 w_scale[32 * q : 32 * q + 4 * PASSES, :].bitcast(I32),
                 w_scales[:, 4 * q : 4 * q + 4, :].bitcast(I32),
             )
-        for part in range(2):
-            cols = slice(part * M // 2, (part + 1) * M // 2)
-            for a in range(PASSES):
-                nc.sync.dma_start(
-                    w_sb[a][part][:].bitcast(I32),
-                    w_words[a, :, cols, :].rearrange("p n i -> p (n i)").bitcast(I32),
-                )
-        load_wgo(1)
+        load_w(w_early, 0, W_EARLY)
+        nc.sync.dma_start(offs2_sb[:], offs2)
+        nc.sync.dma_start(wgo_sb[:], wgo)
+        load_w(w_late, W_EARLY, M)
 
-        def gather(a, i, h):
+        b_psum = psum_b.tile([P, P], F32, name="b_psum")
+        nc.tensor.transpose(b_psum[:], b_rows[:], ident[:])
+        nc.scalar.copy(out=b_col[:], in_=b_psum[:, 0:ROW_TILES])
+        nc.scalar.copy(out=b_first[:], in_=b_psum[:, 0:1])
+
+        def gather(dst, a, i, first, last):
             nc.vector.tensor_tensor(
-                picked[a][h][:, i, :],
-                x_sb[a][i][:].indirect(offs_sb[:, h * OFF_COLS : (h + 1) * OFF_COLS]),
-                wgt_sb[h][:],
+                dst,
+                x_sb[a][i][:].indirect(offs_sb[:, first // 16 : last // 16]),
+                wgt_sb[:, first:last],
                 MULT,
             )
 
-        def interleave(a, h):
+        def gather_last(i, h):
+            gather(picked_last[h][:, i, :], LAST, i, h * HALF, (h + 1) * HALF)
+
+        def interleave(dst, planes):
             nc.scalar.copy(
-                out=grouped[a][:, h * HALF : (h + 1) * HALF, :].rearrange("p (c i) t -> p c t i", i=4),
-                in_=picked[a][h][:].rearrange("p t (c i) -> p c t i", i=4),
+                out=dst.rearrange("p (c i t) -> p c t i", i=4, t=PACK),
+                in_=planes.rearrange("p t (c i) -> p c t i", i=4),
             )
 
-        def quantize(a, first, last):
-            nc.vector.quantize_mx(
-                out=codes[a][:, first:last].bitcast(FP8X4),
-                scales=scales[a][:, first:last],
-                in_=grouped[a][:, first:last, :].rearrange("p c t -> p (c t)"),
-            )
+        def quantize(a, first, last, src):
+            nc.vector.quantize_mx(out=codes[a][:, first:last].bitcast(FP8X4), scales=scales[a][:, first:last], in_=src[:])
+
+        def quantize_last(h):
+            quantize(LAST, h * HALF, (h + 1) * HALF, grouped2[h])
 
         def project(r, first, last):
             acc = psum.tile([P, S], F32, name="acc")
             cols = slice(r * P, (r + 1) * P)
-            part, w_first = divmod(r * P, M // 2)
+            w_tile, w_first = (w_early, r * P) if r < EARLY else (w_late, r * P - W_EARLY)
             for a in range(PASSES):
                 nc.tensor.matmul_mx(
                     out=acc[:, first:last],
-                    lhsT=w_sb[a][part][:, w_first : w_first + P].bitcast(FP8X4),
+                    lhsT=w_tile[:, a, w_first : w_first + P].bitcast(FP8X4),
                     lhsT_scale=w_scale[4 * a :, cols],
                     rhs=codes[a][:, first:last].bitcast(FP8X4),
                     rhs_scale=scales[a][:, first:last],
                     start=(a == 0),
-                    stop=(a == PASSES - 1),
+                    stop=(a == LAST),
                 )
-            nc.scalar.activation(acted[r][:, first:last], acc[:, first:last], GELU, bias=b_col[:, r : r + 1])
+            bias = b_first[:] if (r, first) == (0, 0) else b_col[:, r : r + 1]
+            nc.scalar.activation(acted_cols(r, first, last), acc[:, first:last], GELU, bias=bias)
 
-        def scatter(r, h):
+        def scatter(r, first, last):
             nc.vector.tensor_tensor(
-                windows[r % WINDOWS][:].indirect(offs2_sb[:, h * OFF_COLS : (h + 1) * OFF_COLS]),
-                acted[r][:, h * HALF : (h + 1) * HALF],
-                wgo_sb[h][:],
+                windows[r % WINDOWS][:].indirect(offs2_sb[:, first // 16 : last // 16]),
+                acted_cols(r, first, last),
+                wgo_sb[:, first:last],
                 MULT,
             )
 
         def store(r):
             nc.sync.dma_start(out[r * P : (r + 1) * P, :], windows[r % WINDOWS][:])
 
+        for a in range(LAST):
+            for i in range(PACK):
+                gather(picked[a][:, i, :], a, i, 0, S)
+            interleave(grouped[a][:], picked[a][:])
+        quantize(0, 0, S, grouped[0])
         for i in range(PACK):
-            gather(0, i, 0)
-            gather(0, i, 1)
-        interleave(0, 0)
-        interleave(0, 1)
-        for i in range(PACK):
-            gather(1, i, 0)
-        interleave(1, 0)
-        quantize(0, 0, S)
-        for i in range(PACK):
-            gather(1, i, 1)
-        interleave(1, 1)
-        nc.vector.transpose(b_col[:], b_rows[:])
-        for i in range(PACK):
-            gather(2, i, 0)
-        interleave(2, 0)
-        quantize(1, 0, S)
-        gather(2, 0, 1)
-        gather(2, 1, 1)
-        quantize(2, 0, HALF)
+            gather_last(i, 0)
+            if i == 1:
+                gather_last(i, 1)
+        interleave(grouped2[0][:], picked_last[0])
+        gather_last(0, 1)
+        quantize(1, 0, S, grouped[1])
+        quantize_last(0)
         project(0, 0, HALF)
+        gather_last(2, 1)
+        gather_last(3, 1)
+        interleave(grouped2[1][:], picked_last[1])
+        scatter(0, 0, HALF)
         project(1, 0, HALF)
-        gather(2, 2, 1)
-        gather(2, 3, 1)
-        interleave(2, 1)
-        scatter(0, 0)
-        project(2, 0, HALF)
-        project(3, 0, HALF)
-        scatter(1, 0)
-        quantize(2, HALF, S)
-        project(0, HALF, S)
-        project(1, HALF, S)
-        scatter(2, 0)
-        scatter(3, 0)
-        scatter(0, 1)
-        store(0)
-        scatter(1, 1)
-        store(1)
-        project(2, HALF, S)
-        project(3, HALF, S)
-        scatter(2, 1)
-        store(2)
-        scatter(3, 1)
-        store(3)
-        for r in range(4, ROW_TILES, 2):
-            project(r, 0, S)
-            project(r + 1, 0, S)
-            scatter(r, 0)
-            scatter(r + 1, 0)
-            scatter(r, 1)
+        quantize_last(1)
+        scatter(1, 0, HALF)
+        for r in range(EARLY):
+            project(r, HALF, S)
+            scatter(r, HALF, S)
             store(r)
-            scatter(r + 1, 1)
-            store(r + 1)
+        for r in range(EARLY, ROW_TILES):
+            project(r, 0, S)
+            scatter(r, 0, S)
+            store(r)

@@ -37,29 +37,29 @@ def tile_list_hboth_gelu_kernel(tc, xT, w_words, w_scales, wgt, b, wgo, offs, of
 
         offs_sb = keep.tile([P, S // 16], U16, name="offs_sb")
         offs2_sb = keep.tile([P, S // 16], U16, name="offs2_sb")
-        slots = keep.tile([P, 8, HALF], F32, name="slots")
+        slots = keep.tile([P, 7, HALF], F32, name="slots")
         wgt_sb = slots[:, 0:2, :].rearrange("p h c -> p (h c)")
-        picked_last = [slots[:, 4:8, :], slots[:, 0:8:2, :]]
+        picked_last = [slots[:, 2:6, :], slots[:, 0:7:2, :]]
         wgo_sb = keep.tile([P, S], F32, name="wgo_sb")
         x_sb = [[keep.tile([P, T], F32, align_bytes=64, name=f"x{a}_{i}", tag=f"x{a}_{i}") for i in range(PACK)] for a in range(PASSES)]
         w_early = keep.tile([P, PASSES, W_EARLY], U32, align_bytes=64, name="w_early")
         w_late = keep.tile([P, PASSES, M - W_EARLY], U32, align_bytes=64, name="w_late")
         w_scale = keep.tile([P, M], U8, align_bytes=64, name="w_scale")
         ident = keep.tile([P, P], F32, name="ident")
-        b_rows = keep.tile([P, P], F32, name="b_rows")
+        b_rows = keep.tile([P, P], F32, align_bytes=64, name="b_rows", tag="b_rows")
         b_col = keep.tile([P, ROW_TILES], F32, name="b_col")
         warm = keep.tile([P, 1], F32, name="warm")
         windows = [keep.tile([P, T], F32, name=f"window{r}") for r in range(WINDOWS)]
         picked = [keep.tile([P, PACK, S], F32, name=f"picked{a}") for a in range(LAST)]
-        grouped = [keep.tile([P, S * PACK], BF16, align_bytes=64, name=f"grouped{a}") for a in range(LAST)]
+        grouped01 = keep.tile([P, LAST * S * PACK], BF16, align_bytes=64, name="grouped01")
         b_first = keep.tile([P, 1], F32, align_bytes=64, name="b_first", tag="grouped2_1")
         grouped2 = [keep.tile([P, HALF * PACK], BF16, align_bytes=64, name=f"grouped2_{h}", tag=f"grouped2_{h}") for h in range(2)]
-        codes = [
-            keep.tile([P, S], U32, align_bytes=64, name="codes0"),
-            keep.tile([P, S], U32, align_bytes=64, name="codes1", tag="x2_0"),
-            keep.tile([P, S], U32, align_bytes=64, name="codes2"),
-        ]
-        scales = [keep.tile([P, S], U8, align_bytes=64, name=f"scales{a}") for a in range(PASSES)]
+        codes01 = keep.tile([P, LAST * S], U32, align_bytes=64, name="codes01")
+        scales01 = keep.tile([P, LAST * S], U8, align_bytes=64, name="scales01", tag="b_rows")
+        codes2 = keep.tile([P, S], U32, align_bytes=64, name="codes2")
+        scales2 = keep.tile([P, S], U8, align_bytes=64, name="scales2")
+        codes = [codes01[:, 0:S], codes01[:, S : 2 * S], codes2[:]]
+        scales = [scales01[:, 0:S], scales01[:, S : 2 * S], scales2[:]]
         acted = [keep.tile([P, S], F32, name=f"acted{r}") for r in range(ROW_TILES)]
 
         def acted_cols(r, first, last):
@@ -93,7 +93,7 @@ def tile_list_hboth_gelu_kernel(tc, xT, w_words, w_scales, wgt, b, wgo, offs, of
             for i in range(PACK):
                 if (a, i) != (0, 0):
                     load_x(a, i)
-            if a == 0:
+            if a == LAST:
                 nc.sync.dma_start(b_rows[0:ROW_TILES, :], b.rearrange("(r p) -> r p", p=P))
         for q in range(4):
             nc.sync.dma_start(
@@ -164,19 +164,17 @@ def tile_list_hboth_gelu_kernel(tc, xT, w_words, w_scales, wgt, b, wgo, offs, of
         for a in range(LAST):
             for i in range(PACK):
                 gather(picked[a][:, i, :], a, i, 0, S)
-            interleave(grouped[a][:], picked[a][:])
-        quantize(0, 0, S, grouped[0])
-        for i in range(PACK):
+            interleave(grouped01[:, a * S * PACK : (a + 1) * S * PACK], picked[a][:])
+        for i in range(PACK - 1):
             gather_last(i, 0)
-            if i == 1:
-                gather_last(i, 1)
+        gather(slots[:, 5:7, :].rearrange("p h c -> p (h c)"), LAST, PACK - 1, 0, S)
         interleave(grouped2[0][:], picked_last[0])
+        nc.vector.quantize_mx(out=codes01[:].bitcast(FP8X4), scales=scales01[:], in_=grouped01[:])
         gather_last(0, 1)
-        quantize(1, 0, S, grouped[1])
         quantize_last(0)
         project(0, 0, HALF)
+        gather_last(1, 1)
         gather_last(2, 1)
-        gather_last(3, 1)
         interleave(grouped2[1][:], picked_last[1])
         scatter(0, 0, HALF)
         project(1, 0, HALF)

@@ -19,10 +19,10 @@ PACK = 4
 PASSES = K // (P * PACK)
 LAST = PASSES - 1
 ROW_TILES = M // P
-WINDOWS = 3
+WINDOWS = 4
 HALF = S // 2
 OFF_COLS = HALF // 16
-EARLY = 2
+EARLY = 3
 W_EARLY = EARLY * P
 
 FLOPS = 2 * K * M * S
@@ -37,9 +37,9 @@ def tile_list_hboth_gelu_kernel(tc, xT, w_words, w_scales, wgt, b, wgo, offs, of
 
         offs_sb = keep.tile([P, S // 16], U16, name="offs_sb")
         offs2_sb = keep.tile([P, S // 16], U16, name="offs2_sb")
-        slots = keep.tile([P, 7, HALF], F32, name="slots")
+        slots = keep.tile([P, 9, HALF], F32, name="slots")
         wgt_sb = slots[:, 0:2, :].rearrange("p h c -> p (h c)")
-        picked_last = [slots[:, 2:6, :], slots[:, 0:7:2, :]]
+        picked_last = [slots[:, 2:9:2, :], slots[:, 0:7:2, :]]
         wgo_sb = keep.tile([P, S], F32, name="wgo_sb")
         x_sb = [[keep.tile([P, T], F32, align_bytes=64, name=f"x{a}_{i}", tag=f"x{a}_{i}") for i in range(PACK)] for a in range(PASSES)]
         w_early = keep.tile([P, PASSES, W_EARLY], U32, align_bytes=64, name="w_early")
@@ -63,7 +63,7 @@ def tile_list_hboth_gelu_kernel(tc, xT, w_words, w_scales, wgt, b, wgo, offs, of
         acted = [keep.tile([P, S], F32, name=f"acted{r}") for r in range(ROW_TILES)]
 
         def acted_cols(r, first, last):
-            if (r, first) == (1, 0):
+            if (r, first) == (EARLY - 1, 0):
                 return slots[:, 2, :]
             return acted[r][:, first:last]
 
@@ -83,8 +83,9 @@ def tile_list_hboth_gelu_kernel(tc, xT, w_words, w_scales, wgt, b, wgo, offs, of
         nc.vector.memset(w_scale[:].bitcast(I32), 0)
 
         make_identity(nc, ident[:])
-        for window in windows:
-            nc.gpsimd.memset(window[:].bitcast(I32), 0)
+        for r, window in enumerate(windows):
+            engine = nc.vector if r < EARLY else nc.gpsimd
+            engine.memset(window[:].bitcast(I32), 0)
 
         nc.sync.dma_start(offs_sb[:], offs)
         load_x(0, 0)
@@ -159,27 +160,35 @@ def tile_list_hboth_gelu_kernel(tc, xT, w_words, w_scales, wgt, b, wgo, offs, of
             )
 
         def store(r):
-            nc.sync.dma_start(out[r * P : (r + 1) * P, :], windows[r % WINDOWS][:])
+            rows = out[r * P : (r + 1) * P, :]
+            window = windows[r % WINDOWS]
+            if r < ROW_TILES - 1:
+                nc.sync.dma_start(rows, window[:])
+            else:
+                nc.sync.dma_start(rows[:, 0 : T // 2], window[:, 0 : T // 2])
+                nc.scalar.dma_start(rows[:, T // 2 : T], window[:, T // 2 : T])
 
         for a in range(LAST):
             for i in range(PACK):
                 gather(picked[a][:, i, :], a, i, 0, S)
             interleave(grouped01[:, a * S * PACK : (a + 1) * S * PACK], picked[a][:])
-        for i in range(PACK - 1):
+        for i in range(PACK):
             gather_last(i, 0)
-        gather(slots[:, 5:7, :].rearrange("p h c -> p (h c)"), LAST, PACK - 1, 0, S)
         interleave(grouped2[0][:], picked_last[0])
         nc.vector.quantize_mx(out=codes01[:].bitcast(FP8X4), scales=scales01[:], in_=grouped01[:])
         gather_last(0, 1)
         quantize_last(0)
         project(0, 0, HALF)
+        project(1, 0, HALF)
         gather_last(1, 1)
         gather_last(2, 1)
+        gather_last(3, 1)
         interleave(grouped2[1][:], picked_last[1])
         scatter(0, 0, HALF)
-        project(1, 0, HALF)
-        quantize_last(1)
         scatter(1, 0, HALF)
+        project(2, 0, HALF)
+        quantize_last(1)
+        scatter(2, 0, HALF)
         for r in range(EARLY):
             project(r, HALF, S)
             scatter(r, HALF, S)

@@ -19,11 +19,12 @@ PACK = 4
 PASSES = K // (P * PACK)
 LAST = PASSES - 1
 ROW_TILES = M // P
-WINDOWS = 4
-HALF = S // 2
-OFF_COLS = HALF // 16
-EARLY = 3
-W_EARLY = EARLY * P
+LEAD = 128
+REST = S - LEAD
+EARLY = 5
+AHEAD = 3
+WINDOWS = EARLY
+W_CUTS = (0, 2, EARLY, ROW_TILES)
 
 FLOPS = 2 * K * M * S
 
@@ -37,13 +38,13 @@ def tile_list_hboth_gelu_kernel(tc, xT, w_words, w_scales, wgt, b, wgo, offs, of
 
         offs_sb = keep.tile([P, S // 16], U16, name="offs_sb")
         offs2_sb = keep.tile([P, S // 16], U16, name="offs2_sb")
-        slots = keep.tile([P, 9, HALF], F32, name="slots")
-        wgt_sb = slots[:, 0:2, :].rearrange("p h c -> p (h c)")
-        picked_last = [slots[:, 2:9:2, :], slots[:, 0:7:2, :]]
+        wgt_sb = keep.tile([P, S], F32, name="wgt_sb")
         wgo_sb = keep.tile([P, S], F32, name="wgo_sb")
-        x_sb = [[keep.tile([P, T], F32, align_bytes=64, name=f"x{a}_{i}", tag=f"x{a}_{i}") for i in range(PACK)] for a in range(PASSES)]
-        w_early = keep.tile([P, PASSES, W_EARLY], U32, align_bytes=64, name="w_early")
-        w_late = keep.tile([P, PASSES, M - W_EARLY], U32, align_bytes=64, name="w_late")
+        x_sb = [[keep.tile([P, T], F32, name=f"x{a}_{i}") for i in range(PACK)] for a in range(PASSES)]
+        w_sb = [
+            keep.tile([P, PASSES, (W_CUTS[n + 1] - W_CUTS[n]) * P], U32, align_bytes=64, name=f"w{n}")
+            for n in range(len(W_CUTS) - 1)
+        ]
         w_scale = keep.tile([P, M], U8, align_bytes=64, name="w_scale")
         ident = keep.tile([P, P], F32, name="ident")
         b_rows = keep.tile([P, P], F32, align_bytes=64, name="b_rows", tag="b_rows")
@@ -51,9 +52,13 @@ def tile_list_hboth_gelu_kernel(tc, xT, w_words, w_scales, wgt, b, wgo, offs, of
         warm = keep.tile([P, 1], F32, name="warm")
         windows = [keep.tile([P, T], F32, name=f"window{r}") for r in range(WINDOWS)]
         picked = [keep.tile([P, PACK, S], F32, name=f"picked{a}") for a in range(LAST)]
+        last = keep.tile([P, PACK * 5 * LEAD], F32, name="last")
+        last_lead = last[:].rearrange("p (i c) -> p i c", i=PACK)[:, :, 0:LEAD]
+        last_rest = last[:, 2 * LEAD : 2 * LEAD + PACK * S].rearrange("p (i c) -> p i c", i=PACK)[:, :, 0:REST]
         grouped01 = keep.tile([P, LAST * S * PACK], BF16, align_bytes=64, name="grouped01")
-        b_first = keep.tile([P, 1], F32, align_bytes=64, name="b_first", tag="grouped2_1")
-        grouped2 = [keep.tile([P, HALF * PACK], BF16, align_bytes=64, name=f"grouped2_{h}", tag=f"grouped2_{h}") for h in range(2)]
+        grouped_lead = keep.tile([P, LEAD * PACK], BF16, align_bytes=64, name="grouped_lead")
+        b_held = keep.tile([P, 1], F32, align_bytes=64, name="b_held", tag="grouped_rest")
+        grouped_rest = keep.tile([P, REST * PACK], BF16, align_bytes=64, name="grouped_rest", tag="grouped_rest")
         codes01 = keep.tile([P, LAST * S], U32, align_bytes=64, name="codes01")
         scales01 = keep.tile([P, LAST * S], U8, align_bytes=64, name="scales01", tag="b_rows")
         codes2 = keep.tile([P, S], U32, align_bytes=64, name="codes2")
@@ -62,19 +67,19 @@ def tile_list_hboth_gelu_kernel(tc, xT, w_words, w_scales, wgt, b, wgo, offs, of
         scales = [scales01[:, 0:S], scales01[:, S : 2 * S], scales2[:]]
         acted = [keep.tile([P, S], F32, name=f"acted{r}") for r in range(ROW_TILES)]
 
-        def acted_cols(r, first, last):
-            if (r, first) == (EARLY - 1, 0):
-                return slots[:, 2, :]
-            return acted[r][:, first:last]
+        def acted_cols(r, first, end):
+            if AHEAD <= r < EARLY and first == 0:
+                return last_rest[:, 0, (r - AHEAD) * LEAD : (r - AHEAD + 1) * LEAD]
+            return acted[r][:, first:end]
 
         def load_x(a, i):
             rows = xT.rearrange("(a p i) t -> a i p t", a=PASSES, i=PACK)
             nc.sync.dma_start(x_sb[a][i][:], rows[a, i])
 
-        def load_w(tile, first, last):
+        def load_w(n):
             nc.sync.dma_start(
-                tile[:].bitcast(I32),
-                w_words[:, :, first:last, :].rearrange("a p n i -> p a (n i)").bitcast(I32),
+                w_sb[n][:].bitcast(I32),
+                w_words[:, :, W_CUTS[n] * P : W_CUTS[n + 1] * P, :].rearrange("a p n i -> p a (n i)").bitcast(I32),
             )
 
         nc.vector.memset(warm[:], 0.0)
@@ -83,44 +88,41 @@ def tile_list_hboth_gelu_kernel(tc, xT, w_words, w_scales, wgt, b, wgo, offs, of
         nc.vector.memset(w_scale[:].bitcast(I32), 0)
 
         make_identity(nc, ident[:])
-        for r, window in enumerate(windows):
-            engine = nc.vector if r < EARLY else nc.gpsimd
-            engine.memset(window[:].bitcast(I32), 0)
+        for window in windows:
+            nc.gpsimd.memset(window[:].bitcast(I32), 0)
 
         nc.sync.dma_start(offs_sb[:], offs)
         load_x(0, 0)
-        nc.sync.dma_start(wgt_sb, wgt)
+        nc.sync.dma_start(wgt_sb[:], wgt)
         for a in range(PASSES):
             for i in range(PACK):
                 if (a, i) != (0, 0):
                     load_x(a, i)
-            if a == LAST:
-                nc.sync.dma_start(b_rows[0:ROW_TILES, :], b.rearrange("(r p) -> r p", p=P))
+        nc.sync.dma_start(b_rows[0:ROW_TILES, :], b.rearrange("(r p) -> r p", p=P))
         for q in range(4):
             nc.sync.dma_start(
                 w_scale[32 * q : 32 * q + 4 * PASSES, :].bitcast(I32),
                 w_scales[:, 4 * q : 4 * q + 4, :].bitcast(I32),
             )
-        load_w(w_early, 0, W_EARLY)
+        load_w(0)
         nc.sync.dma_start(offs2_sb[:], offs2)
-        nc.sync.dma_start(wgo_sb[:], wgo)
-        load_w(w_late, W_EARLY, M)
+        nc.sync.dma_start(wgo_sb[:, 0:LEAD], wgo[:, 0:LEAD])
+        load_w(1)
+        nc.sync.dma_start(wgo_sb[:, LEAD:S], wgo[:, LEAD:S])
+        load_w(2)
 
         b_psum = psum_b.tile([P, P], F32, name="b_psum")
         nc.tensor.transpose(b_psum[:], b_rows[:], ident[:])
         nc.scalar.copy(out=b_col[:], in_=b_psum[:, 0:ROW_TILES])
-        nc.scalar.copy(out=b_first[:], in_=b_psum[:, 0:1])
+        nc.scalar.copy(out=b_held[:], in_=b_psum[:, AHEAD - 1 : AHEAD])
 
-        def gather(dst, a, i, first, last):
+        def gather(dst, a, i, first, end):
             nc.vector.tensor_tensor(
                 dst,
-                x_sb[a][i][:].indirect(offs_sb[:, first // 16 : last // 16]),
-                wgt_sb[:, first:last],
+                x_sb[a][i][:].indirect(offs_sb[:, first // 16 : end // 16]),
+                wgt_sb[:, first:end],
                 MULT,
             )
-
-        def gather_last(i, h):
-            gather(picked_last[h][:, i, :], LAST, i, h * HALF, (h + 1) * HALF)
 
         def interleave(dst, planes):
             nc.scalar.copy(
@@ -128,34 +130,33 @@ def tile_list_hboth_gelu_kernel(tc, xT, w_words, w_scales, wgt, b, wgo, offs, of
                 in_=planes.rearrange("p t (c i) -> p c t i", i=4),
             )
 
-        def quantize(a, first, last, src):
-            nc.vector.quantize_mx(out=codes[a][:, first:last].bitcast(FP8X4), scales=scales[a][:, first:last], in_=src[:])
+        def quantize_last(first, end, src):
+            nc.vector.quantize_mx(out=codes2[:, first:end].bitcast(FP8X4), scales=scales2[:, first:end], in_=src)
 
-        def quantize_last(h):
-            quantize(LAST, h * HALF, (h + 1) * HALF, grouped2[h])
-
-        def project(r, first, last):
+        def project(r, cuts):
             acc = psum.tile([P, S], F32, name="acc")
-            cols = slice(r * P, (r + 1) * P)
-            w_tile, w_first = (w_early, r * P) if r < EARLY else (w_late, r * P - W_EARLY)
-            for a in range(PASSES):
+            n = max(n for n in range(len(W_CUTS) - 1) if W_CUTS[n] <= r)
+            w_first = (r - W_CUTS[n]) * P
+            steps = [(a, cuts[c], cuts[c + 1]) for a in range(PASSES) for c in range(len(cuts) - 1)]
+            for step, (a, first, end) in enumerate(steps):
                 nc.tensor.matmul_mx(
-                    out=acc[:, first:last],
-                    lhsT=w_tile[:, a, w_first : w_first + P].bitcast(FP8X4),
-                    lhsT_scale=w_scale[4 * a :, cols],
-                    rhs=codes[a][:, first:last].bitcast(FP8X4),
-                    rhs_scale=scales[a][:, first:last],
-                    start=(a == 0),
-                    stop=(a == LAST),
+                    out=acc[:, first:end],
+                    lhsT=w_sb[n][:, a, w_first : w_first + P].bitcast(FP8X4),
+                    lhsT_scale=w_scale[4 * a :, r * P : (r + 1) * P],
+                    rhs=codes[a][:, first:end].bitcast(FP8X4),
+                    rhs_scale=scales[a][:, first:end],
+                    start=(step == 0),
+                    stop=(step == len(steps) - 1),
                 )
-            bias = b_first[:] if (r, first) == (0, 0) else b_col[:, r : r + 1]
-            nc.scalar.activation(acted_cols(r, first, last), acc[:, first:last], GELU, bias=bias)
+            first, end = cuts[0], cuts[-1]
+            bias = b_held[:] if (r, first) == (AHEAD - 1, 0) else b_col[:, r : r + 1]
+            nc.scalar.activation(acted_cols(r, first, end), acc[:, first:end], GELU, bias=bias)
 
-        def scatter(r, first, last):
+        def scatter(r, first, end):
             nc.vector.tensor_tensor(
-                windows[r % WINDOWS][:].indirect(offs2_sb[:, first // 16 : last // 16]),
-                acted_cols(r, first, last),
-                wgo_sb[:, first:last],
+                windows[r % WINDOWS][:].indirect(offs2_sb[:, first // 16 : end // 16]),
+                acted_cols(r, first, end),
+                wgo_sb[:, first:end],
                 MULT,
             )
 
@@ -172,28 +173,32 @@ def tile_list_hboth_gelu_kernel(tc, xT, w_words, w_scales, wgt, b, wgo, offs, of
             for i in range(PACK):
                 gather(picked[a][:, i, :], a, i, 0, S)
             interleave(grouped01[:, a * S * PACK : (a + 1) * S * PACK], picked[a][:])
-        for i in range(PACK):
-            gather_last(i, 0)
-        interleave(grouped2[0][:], picked_last[0])
+        gather(last_lead[:, 0, :], LAST, 0, 0, LEAD)
+        gather(last_rest[:, 0, :], LAST, 0, LEAD, S)
+        gather(last[:, 5 * LEAD : 5 * LEAD + S], LAST, 1, 0, S)
+        gather(last_lead[:, 2, :], LAST, 2, 0, LEAD)
+        gather(last_lead[:, 3, :], LAST, 3, 0, LEAD)
+        interleave(grouped_lead[:], last_lead)
         nc.vector.quantize_mx(out=codes01[:].bitcast(FP8X4), scales=scales01[:], in_=grouped01[:])
-        gather_last(0, 1)
-        quantize_last(0)
-        project(0, 0, HALF)
-        project(1, 0, HALF)
-        gather_last(1, 1)
-        gather_last(2, 1)
-        gather_last(3, 1)
-        interleave(grouped2[1][:], picked_last[1])
-        scatter(0, 0, HALF)
-        scatter(1, 0, HALF)
-        project(2, 0, HALF)
-        quantize_last(1)
-        scatter(2, 0, HALF)
+        quantize_last(0, LEAD, grouped_lead[:])
+        for r in range(AHEAD):
+            project(r, (0, LEAD))
+        gather(last_rest[:, 2, :], LAST, 2, LEAD, S)
+        gather(last_rest[:, 3, :], LAST, 3, LEAD, S)
+        interleave(grouped_rest[:], last_rest)
+        for r in range(AHEAD):
+            scatter(r, 0, LEAD)
+        for r in range(AHEAD, EARLY):
+            project(r, (0, LEAD))
+        quantize_last(LEAD, 2 * LEAD, grouped_rest[:, 0 : LEAD * PACK])
+        quantize_last(2 * LEAD, S, grouped_rest[:, LEAD * PACK : REST * PACK])
+        for r in range(AHEAD, EARLY):
+            scatter(r, 0, LEAD)
         for r in range(EARLY):
-            project(r, HALF, S)
-            scatter(r, HALF, S)
+            project(r, (LEAD, 2 * LEAD, S))
+            scatter(r, LEAD, S)
             store(r)
         for r in range(EARLY, ROW_TILES):
-            project(r, 0, S)
+            project(r, (0, S))
             scatter(r, 0, S)
             store(r)

@@ -24,7 +24,7 @@ REST = S - LEAD
 EARLY = 5
 AHEAD = 3
 WINDOWS = EARLY
-W_CUTS = (0, 2, EARLY, ROW_TILES)
+W_CUTS = (0, 1, AHEAD, EARLY, ROW_TILES)
 
 FLOPS = 2 * K * M * S
 
@@ -52,9 +52,9 @@ def tile_list_hboth_gelu_kernel(tc, xT, w_words, w_scales, wgt, b, wgo, offs, of
         warm = keep.tile([P, 1], F32, name="warm")
         windows = [keep.tile([P, T], F32, name=f"window{r}") for r in range(WINDOWS)]
         picked = [keep.tile([P, PACK, S], F32, name=f"picked{a}") for a in range(LAST)]
-        last = keep.tile([P, PACK * 5 * LEAD], F32, name="last")
-        last_lead = last[:].rearrange("p (i c) -> p i c", i=PACK)[:, :, 0:LEAD]
-        last_rest = last[:, 2 * LEAD : 2 * LEAD + PACK * S].rearrange("p (i c) -> p i c", i=PACK)[:, :, 0:REST]
+        last = keep.tile([P, 2 * (2 * S + LEAD)], F32, name="last")
+        last_lead = last[:].rearrange("p (u x) -> p u x", u=2)[:, :, 0 : 2 * S].rearrange("p u (v c) -> p u v c", v=2)[:, :, :, 0:LEAD]
+        last_rest = last[:, 0 : PACK * S].rearrange("p (i c) -> p i c", i=PACK)[:, :, LEAD:S]
         grouped01 = keep.tile([P, LAST * S * PACK], BF16, align_bytes=64, name="grouped01")
         grouped_lead = keep.tile([P, LEAD * PACK], BF16, align_bytes=64, name="grouped_lead")
         b_held = keep.tile([P, 1], F32, align_bytes=64, name="b_held", tag="grouped_rest")
@@ -105,11 +105,12 @@ def tile_list_hboth_gelu_kernel(tc, xT, w_words, w_scales, wgt, b, wgo, offs, of
                 w_scales[:, 4 * q : 4 * q + 4, :].bitcast(I32),
             )
         load_w(0)
+        load_w(1)
         nc.sync.dma_start(offs2_sb[:], offs2)
         nc.sync.dma_start(wgo_sb[:, 0:LEAD], wgo[:, 0:LEAD])
-        load_w(1)
-        nc.sync.dma_start(wgo_sb[:, LEAD:S], wgo[:, LEAD:S])
         load_w(2)
+        nc.sync.dma_start(wgo_sb[:, LEAD:S], wgo[:, LEAD:S])
+        load_w(3)
 
         b_psum = psum_b.tile([P, P], F32, name="b_psum")
         nc.tensor.transpose(b_psum[:], b_rows[:], ident[:])
@@ -163,22 +164,22 @@ def tile_list_hboth_gelu_kernel(tc, xT, w_words, w_scales, wgt, b, wgo, offs, of
         def store(r):
             rows = out[r * P : (r + 1) * P, :]
             window = windows[r % WINDOWS]
-            if r < ROW_TILES - 1:
-                nc.sync.dma_start(rows, window[:])
-            else:
-                nc.sync.dma_start(rows[:, 0 : T // 2], window[:, 0 : T // 2])
-                nc.scalar.dma_start(rows[:, T // 2 : T], window[:, T // 2 : T])
+            nc.sync.dma_start(rows[:, 0 : T // 2], window[:, 0 : T // 2])
+            second = nc.scalar if r == ROW_TILES - 1 else nc.sync
+            second.dma_start(rows[:, T // 2 : T], window[:, T // 2 : T])
 
         for a in range(LAST):
             for i in range(PACK):
                 gather(picked[a][:, i, :], a, i, 0, S)
             interleave(grouped01[:, a * S * PACK : (a + 1) * S * PACK], picked[a][:])
-        gather(last_lead[:, 0, :], LAST, 0, 0, LEAD)
-        gather(last_rest[:, 0, :], LAST, 0, LEAD, S)
-        gather(last[:, 5 * LEAD : 5 * LEAD + S], LAST, 1, 0, S)
-        gather(last_lead[:, 2, :], LAST, 2, 0, LEAD)
-        gather(last_lead[:, 3, :], LAST, 3, 0, LEAD)
-        interleave(grouped_lead[:], last_lead)
+        for i in range(2):
+            gather(last[:, i * S : (i + 1) * S], LAST, i, 0, S)
+        for i in range(2):
+            gather(last_lead[:, 1, i, :], LAST, 2 + i, 0, LEAD)
+        nc.scalar.copy(
+            out=grouped_lead[:].rearrange("p (c i u v) -> p c u v i", i=4, u=2, v=2),
+            in_=last_lead.rearrange("p u v (c i) -> p c u v i", i=4),
+        )
         nc.vector.quantize_mx(out=codes01[:].bitcast(FP8X4), scales=scales01[:], in_=grouped01[:])
         quantize_last(0, LEAD, grouped_lead[:])
         for r in range(AHEAD):

@@ -191,12 +191,12 @@ def tile_list_hboth_gelu_kernel(tc, xT, w_words, w_scales, wgt, b, wgo, offs, of
             scatter(r, 0, LEAD)
         for r in range(AHEAD, EARLY):
             project(r, (0, LEAD))
-        quantize_last(LEAD, 2 * LEAD, grouped_rest[:, 0 : LEAD * PACK])
-        quantize_last(2 * LEAD, S, grouped_rest[:, LEAD * PACK : REST * PACK])
+        quantize_last(LEAD, S - LEAD, grouped_rest[:, 0 : (REST - LEAD) * PACK])
+        quantize_last(S - LEAD, S, grouped_rest[:, (REST - LEAD) * PACK : REST * PACK])
         for r in range(AHEAD, EARLY):
             scatter(r, 0, LEAD)
         for r in range(EARLY):
-            project(r, (LEAD, 2 * LEAD, S))
+            project(r, (LEAD, S - LEAD, S))
             scatter(r, LEAD, S)
             store(r)
         for r in range(EARLY, ROW_TILES):

@@ -91,8 +91,8 @@ def tile_list_hboth_gelu_kernel(tc, xT, w_words, w_scales, wgt, b, wgo, offs, of
         for window in windows:
             nc.gpsimd.memset(window[:].bitcast(I32), 0)
 
-        nc.sync.dma_start(offs_sb[:], offs)
         load_x(0, 0)
+        nc.sync.dma_start(offs_sb[:], offs)
         nc.sync.dma_start(wgt_sb[:], wgt)
         for a in range(PASSES):
             for i in range(PACK):

@@ -16,6 +16,8 @@ GELU = mybir.ActivationFunctionType.Gelu_apprx_tanh
 K, M, T, S = 1536, 1024, 1024, 512
 P = 128
 PACK = 4
+GROUP = 16
+BLOCK = 32
 PASSES = K // (P * PACK)
 LAST = PASSES - 1
 ROW_TILES = M // P
@@ -38,9 +40,12 @@ def tile_list_hboth_gelu_kernel(tc, xT, w_words, w_scales, wgt, b, wgo, offs, of
 
         offs_sb = keep.tile([P, S // 16], U16, name="offs_sb")
         offs2_sb = keep.tile([P, S // 16], U16, name="offs2_sb")
-        wgt_sb = keep.tile([P, S], F32, name="wgt_sb")
+        wgt_cut = keep.tile([P, BLOCK], F32, align_bytes=64, name="wgt_cut")
+        wgt_turned = keep.tile([P, BLOCK], F32, align_bytes=64, name="wgt_turned")
+        wgt_wide = keep.tile([P, S], F32, align_bytes=64, name="wgt_wide")
+        wgt_sb = keep.tile([P, S], F32, align_bytes=64, name="wgt_sb")
         wgo_sb = keep.tile([P, S], F32, name="wgo_sb")
-        x_sb = [[keep.tile([P, T], F32, name=f"x{a}_{i}") for i in range(PACK)] for a in range(PASSES)]
+        x_sb = [[keep.tile([P, T], F32, name=f"x{a}_{i}", tag=f"x{PACK * a + i}") for i in range(PACK)] for a in range(PASSES)]
         w_sb = [
             keep.tile([P, PASSES, (W_CUTS[n + 1] - W_CUTS[n]) * P], U32, align_bytes=64, name=f"w{n}")
             for n in range(len(W_CUTS) - 1)
@@ -50,7 +55,7 @@ def tile_list_hboth_gelu_kernel(tc, xT, w_words, w_scales, wgt, b, wgo, offs, of
         b_rows = keep.tile([P, P], F32, align_bytes=64, name="b_rows", tag="b_rows")
         b_col = keep.tile([P, ROW_TILES], F32, name="b_col")
         warm = keep.tile([P, 1], F32, name="warm")
-        windows = [keep.tile([P, T], F32, name=f"window{r}") for r in range(WINDOWS)]
+        windows = [keep.tile([P, T], F32, name=f"window{r}", tag=f"x{r}") for r in range(WINDOWS)]
         picked = [keep.tile([P, PACK, S], F32, name=f"picked{a}") for a in range(LAST)]
         last = keep.tile([P, 2 * (2 * S + LEAD)], F32, name="last")
         last_lead = last[:].rearrange("p (u x) -> p u x", u=2)[:, :, 0 : 2 * S].rearrange("p u (v c) -> p u v c", v=2)[:, :, :, 0:LEAD]
@@ -82,18 +87,18 @@ def tile_list_hboth_gelu_kernel(tc, xT, w_words, w_scales, wgt, b, wgo, offs, of
                 w_words[:, :, W_CUTS[n] * P : W_CUTS[n + 1] * P, :].rearrange("a p n i -> p a (n i)").bitcast(I32),
             )
 
+        nc.sync.dma_start(
+            wgt_cut[:], wgt.rearrange("(g r) (s c) -> r g s c", r=GROUP, c=BLOCK)[0]
+        )
         nc.vector.memset(warm[:], 0.0)
         nc.scalar.activation(warm[:], warm[:], GELU)
         nc.vector.memset(b_rows[:], 0.0)
         nc.vector.memset(w_scale[:].bitcast(I32), 0)
 
         make_identity(nc, ident[:])
-        for window in windows:
-            nc.gpsimd.memset(window[:].bitcast(I32), 0)
 
         load_x(0, 0)
         nc.sync.dma_start(offs_sb[:], offs)
-        nc.sync.dma_start(wgt_sb[:], wgt)
         for a in range(PASSES):
             for i in range(PACK):
                 if (a, i) != (0, 0):
@@ -111,6 +116,19 @@ def tile_list_hboth_gelu_kernel(tc, xT, w_words, w_scales, wgt, b, wgo, offs, of
         load_w(2)
         nc.sync.dma_start(wgo_sb[:, LEAD:S], wgo[:, LEAD:S])
         load_w(3)
+
+        nc.vector.transpose(wgt_turned[:], wgt_cut[:])
+        halves = [slice(0, S // 2), slice(S // 2, S)]
+        for u, cols in enumerate(halves):
+            nc.vector.tensor_copy(
+                wgt_wide[:, cols].rearrange("p (s h r) -> p s h r", h=2, r=GROUP),
+                wgt_turned[:]
+                .rearrange("p (h u s) -> p u s h", h=2, u=2)[:, u]
+                .unsqueeze(3)
+                .to_broadcast([P, GROUP // 2, 2, GROUP]),
+            )
+        for cols in halves:
+            nc.vector.transpose(wgt_sb[:, cols], wgt_wide[:, cols])
 
         b_psum = psum_b.tile([P, P], F32, name="b_psum")
         nc.tensor.transpose(b_psum[:], b_rows[:], ident[:])
@@ -171,6 +189,8 @@ def tile_list_hboth_gelu_kernel(tc, xT, w_words, w_scales, wgt, b, wgo, offs, of
         for a in range(LAST):
             for i in range(PACK):
                 gather(picked[a][:, i, :], a, i, 0, S)
+                if PACK * a + i < WINDOWS:
+                    nc.gpsimd.memset(windows[PACK * a + i][:].bitcast(I32), 0)
             interleave(grouped01[:, a * S * PACK : (a + 1) * S * PACK], picked[a][:])
         for i in range(2):
             gather(last[:, i * S : (i + 1) * S], LAST, i, 0, S)

@@ -88,7 +88,7 @@ def tile_list_hboth_gelu_kernel(tc, xT, w_words, w_scales, wgt, b, wgo, offs, of
             )
 
         nc.sync.dma_start(
-            wgt_cut[:], wgt.rearrange("(g r) (s c) -> r g s c", r=GROUP, c=BLOCK)[0]
+            wgt_cut[:], wgt.rearrange("r (h x) -> (r h) x", h=2)[0 : 2 * P : GROUP + 1, :].rearrange("u (v c) -> u v c", c=BLOCK)
         )
         nc.vector.memset(warm[:], 0.0)
         nc.scalar.activation(warm[:], warm[:], GELU)

@@ -45,7 +45,7 @@ def tile_list_hboth_gelu_kernel(tc, xT, w_words, w_scales, wgt, b, wgo, offs, of
         wgt_wide = keep.tile([P, S], F32, align_bytes=64, name="wgt_wide")
         wgt_sb = keep.tile([P, S], F32, align_bytes=64, name="wgt_sb")
         wgo_sb = keep.tile([P, S], F32, name="wgo_sb")
-        x_sb = [[keep.tile([P, T], F32, name=f"x{a}_{i}", tag=f"x{PACK * a + i}") for i in range(PACK)] for a in range(PASSES)]
+        x_sb = [[keep.tile([P, T], F32, align_bytes=64, name=f"x{a}_{i}", tag=f"x{PACK * a + i}") for i in range(PACK)] for a in range(PASSES)]
         w_sb = [
             keep.tile([P, PASSES, (W_CUTS[n + 1] - W_CUTS[n]) * P], U32, align_bytes=64, name=f"w{n}")
             for n in range(len(W_CUTS) - 1)
@@ -55,7 +55,8 @@ def tile_list_hboth_gelu_kernel(tc, xT, w_words, w_scales, wgt, b, wgo, offs, of
         b_rows = keep.tile([P, P], F32, align_bytes=64, name="b_rows", tag="b_rows")
         b_col = keep.tile([P, ROW_TILES], F32, name="b_col")
         warm = keep.tile([P, 1], F32, name="warm")
-        windows = [keep.tile([P, T], F32, name=f"window{r}", tag=f"x{r}") for r in range(WINDOWS)]
+        window_slots = ["window0", "wgt_turned"] + [f"x{n}" for n in range(WINDOWS - 2)]
+        windows = [keep.tile([P, T], F32, align_bytes=64, name=f"window{r}", tag=window_slots[r]) for r in range(WINDOWS)]
         picked = [keep.tile([P, PACK, S], F32, name=f"picked{a}") for a in range(LAST)]
         last = keep.tile([P, 2 * (2 * S + LEAD)], F32, name="last")
         last_lead = last[:].rearrange("p (u x) -> p u x", u=2)[:, :, 0 : 2 * S].rearrange("p u (v c) -> p u v c", v=2)[:, :, :, 0:LEAD]
@@ -95,6 +96,8 @@ def tile_list_hboth_gelu_kernel(tc, xT, w_words, w_scales, wgt, b, wgo, offs, of
         nc.vector.memset(b_rows[:], 0.0)
         nc.vector.memset(w_scale[:].bitcast(I32), 0)
 
+        nc.vector.memset(windows[0][:].bitcast(I32), 0)
+
         make_identity(nc, ident[:])
 
         load_x(0, 0)
@@ -127,6 +130,7 @@ def tile_list_hboth_gelu_kernel(tc, xT, w_words, w_scales, wgt, b, wgo, offs, of
                 .unsqueeze(3)
                 .to_broadcast([P, GROUP // 2, 2, GROUP]),
             )
+        nc.gpsimd.memset(windows[1][:].bitcast(I32), 0)
         for cols in halves:
             nc.vector.transpose(wgt_sb[:, cols], wgt_wide[:, cols])
 
@@ -189,8 +193,8 @@ def tile_list_hboth_gelu_kernel(tc, xT, w_words, w_scales, wgt, b, wgo, offs, of
         for a in range(LAST):
             for i in range(PACK):
                 gather(picked[a][:, i, :], a, i, 0, S)
-                if PACK * a + i < WINDOWS:
-                    nc.gpsimd.memset(windows[PACK * a + i][:].bitcast(I32), 0)
+                if PACK * a + i < WINDOWS - 2:
+                    nc.gpsimd.memset(windows[PACK * a + i + 2][:].bitcast(I32), 0)
             interleave(grouped01[:, a * S * PACK : (a + 1) * S * PACK], picked[a][:])
         for i in range(2):
             gather(last[:, i * S : (i + 1) * S], LAST, i, 0, S)

@@ -55,7 +55,7 @@ def tile_list_hboth_gelu_kernel(tc, xT, w_words, w_scales, wgt, b, wgo, offs, of
         b_rows = keep.tile([P, P], F32, align_bytes=64, name="b_rows", tag="b_rows")
         b_col = keep.tile([P, ROW_TILES], F32, name="b_col")
         warm = keep.tile([P, 1], F32, name="warm")
-        window_slots = ["window0", "wgt_turned"] + [f"x{n}" for n in range(WINDOWS - 2)]
+        window_slots = ["window0", "wgt_turned", "x0", f"x{PACK * LAST + 2}", f"x{PACK * LAST + 3}"]
         windows = [keep.tile([P, T], F32, align_bytes=64, name=f"window{r}", tag=window_slots[r]) for r in range(WINDOWS)]
         picked = [keep.tile([P, PACK, S], F32, name=f"picked{a}") for a in range(LAST)]
         last = keep.tile([P, 2 * (2 * S + LEAD)], F32, name="last")
@@ -193,8 +193,8 @@ def tile_list_hboth_gelu_kernel(tc, xT, w_words, w_scales, wgt, b, wgo, offs, of
         for a in range(LAST):
             for i in range(PACK):
                 gather(picked[a][:, i, :], a, i, 0, S)
-                if PACK * a + i < WINDOWS - 2:
-                    nc.gpsimd.memset(windows[PACK * a + i + 2][:].bitcast(I32), 0)
+                if (a, i) == (0, 0):
+                    nc.gpsimd.memset(windows[2][:].bitcast(I32), 0)
             interleave(grouped01[:, a * S * PACK : (a + 1) * S * PACK], picked[a][:])
         for i in range(2):
             gather(last[:, i * S : (i + 1) * S], LAST, i, 0, S)
@@ -208,8 +208,9 @@ def tile_list_hboth_gelu_kernel(tc, xT, w_words, w_scales, wgt, b, wgo, offs, of
         quantize_last(0, LEAD, grouped_lead[:])
         for r in range(AHEAD):
             project(r, (0, LEAD))
-        gather(last_rest[:, 2, :], LAST, 2, LEAD, S)
-        gather(last_rest[:, 3, :], LAST, 3, LEAD, S)
+        for i in (2, 3):
+            gather(last_rest[:, i, :], LAST, i, LEAD, S)
+            nc.gpsimd.memset(windows[AHEAD + i - 2][:].bitcast(I32), 0)
         interleave(grouped_rest[:], last_rest)
         for r in range(AHEAD):
             scatter(r, 0, LEAD)

from contextlib import ExitStack

import concourse.mybir as mybir
from concourse.masks import make_identity

F32 = mybir.dt.float32
BF16 = mybir.dt.bfloat16
I32 = mybir.dt.int32
U32 = mybir.dt.uint32
U16 = mybir.dt.uint16
U8 = mybir.dt.uint8
FP8X4 = mybir.dt.float8_e4m3fn_x4
MULT = mybir.AluOpType.mult
GELU = mybir.ActivationFunctionType.Gelu_apprx_tanh

K, M, T, S = 1536, 1024, 1024, 512
P = 128
PACK = 4
GROUP = 16
BLOCK = 32
PASSES = K // (P * PACK)
LAST = PASSES - 1
ROW_TILES = M // P
LEAD = 128
REST = S - LEAD
EARLY = 5
AHEAD = 3
WINDOWS = EARLY
W_CUTS = (0, 1, AHEAD, EARLY, ROW_TILES)

FLOPS = 2 * K * M * S


def tile_list_hboth_gelu_kernel(tc, xT, w_words, w_scales, wgt, b, wgo, offs, offs2, out):
    nc = tc.nc
    with ExitStack() as ctx:
        keep = ctx.enter_context(tc.tile_pool(name="keep", bufs=1))
        psum = ctx.enter_context(tc.psum_pool(name="psum", bufs=7))
        psum_b = ctx.enter_context(tc.psum_pool(name="psum_b", bufs=1))

        offs_sb = keep.tile([P, S // 16], U16, name="offs_sb")
        offs2_sb = keep.tile([P, S // 16], U16, name="offs2_sb")
        wgt_cut = keep.tile([P, BLOCK], F32, align_bytes=64, name="wgt_cut")
        wgt_turned = keep.tile([P, BLOCK], F32, align_bytes=64, name="wgt_turned")
        wgt_wide = keep.tile([P, S], F32, align_bytes=64, name="wgt_wide")
        wgt_sb = keep.tile([P, S], F32, align_bytes=64, name="wgt_sb")
        wgo_sb = keep.tile([P, S], F32, name="wgo_sb")
        x_sb = [[keep.tile([P, T], F32, align_bytes=64, name=f"x{a}_{i}", tag=f"x{PACK * a + i}") for i in range(PACK)] for a in range(PASSES)]
        w_sb = [
            keep.tile([P, PASSES, (W_CUTS[n + 1] - W_CUTS[n]) * P], U32, align_bytes=64, name=f"w{n}")
            for n in range(len(W_CUTS) - 1)
        ]
        w_scale = keep.tile([P, M], U8, align_bytes=64, name="w_scale")
        ident = keep.tile([P, P], F32, name="ident")
        b_rows = keep.tile([P, P], F32, align_bytes=64, name="b_rows", tag="b_rows")
        b_col = keep.tile([P, ROW_TILES], F32, name="b_col")
        warm = keep.tile([P, 1], F32, name="warm")
        window_slots = ["window0", "wgt_turned", "x0", f"x{PACK * LAST + 2}", f"x{PACK * LAST + 3}"]
        windows = [keep.tile([P, T], F32, align_bytes=64, name=f"window{r}", tag=window_slots[r]) for r in range(WINDOWS)]
        picked = [keep.tile([P, PACK, S], F32, name=f"picked{a}") for a in range(LAST)]
        last = keep.tile([P, 2 * (2 * S + LEAD)], F32, name="last")
        last_lead = last[:].rearrange("p (u x) -> p u x", u=2)[:, :, 0 : 2 * S].rearrange("p u (v c) -> p u v c", v=2)[:, :, :, 0:LEAD]
        last_rest = last[:, 0 : PACK * S].rearrange("p (i c) -> p i c", i=PACK)[:, :, LEAD:S]
        grouped01 = keep.tile([P, LAST * S * PACK], BF16, align_bytes=64, name="grouped01")
        grouped_lead = keep.tile([P, LEAD * PACK], BF16, align_bytes=64, name="grouped_lead")
        b_held = keep.tile([P, 1], F32, align_bytes=64, name="b_held", tag="grouped_rest")
        grouped_rest = keep.tile([P, REST * PACK], BF16, align_bytes=64, name="grouped_rest", tag="grouped_rest")
        codes01 = keep.tile([P, LAST * S], U32, align_bytes=64, name="codes01")
        scales01 = keep.tile([P, LAST * S], U8, align_bytes=64, name="scales01", tag="b_rows")
        codes2 = keep.tile([P, S], U32, align_bytes=64, name="codes2")
        scales2 = keep.tile([P, S], U8, align_bytes=64, name="scales2")
        codes = [codes01[:, 0:S], codes01[:, S : 2 * S], codes2[:]]
        scales = [scales01[:, 0:S], scales01[:, S : 2 * S], scales2[:]]
        acted = [keep.tile([P, S], F32, name=f"acted{r}") for r in range(ROW_TILES)]

        def acted_cols(r, first, end):
            if AHEAD <= r < EARLY and first == 0:
                return last_rest[:, 0, (r - AHEAD) * LEAD : (r - AHEAD + 1) * LEAD]
            return acted[r][:, first:end]

        def load_x(a, i):
            rows = xT.rearrange("(a p i) t -> a i p t", a=PASSES, i=PACK)
            nc.sync.dma_start(x_sb[a][i][:], rows[a, i])

        def load_w(n):
            nc.sync.dma_start(
                w_sb[n][:].bitcast(I32),
                w_words[:, :, W_CUTS[n] * P : W_CUTS[n + 1] * P, :].rearrange("a p n i -> p a (n i)").bitcast(I32),
            )

        nc.sync.dma_start(
            wgt_cut[:], wgt.rearrange("r (h x) -> (r h) x", h=2)[0 : 2 * P : GROUP + 1, :].rearrange("u (v c) -> u v c", c=BLOCK)
        )
        nc.vector.memset(warm[:], 0.0)
        nc.scalar.activation(warm[:], warm[:], GELU)
        nc.vector.memset(b_rows[:], 0.0)
        nc.vector.memset(w_scale[:].bitcast(I32), 0)

        nc.vector.memset(windows[0][:].bitcast(I32), 0)

        make_identity(nc, ident[:])

        load_x(0, 0)
        nc.sync.dma_start(offs_sb[:], offs)
        for a in range(PASSES):
            for i in range(PACK):
                if (a, i) != (0, 0):
                    load_x(a, i)
        nc.sync.dma_start(b_rows[0:ROW_TILES, :], b.rearrange("(r p) -> r p", p=P))
        for q in range(4):
            nc.sync.dma_start(
                w_scale[32 * q : 32 * q + 4 * PASSES, :].bitcast(I32),
                w_scales[:, 4 * q : 4 * q + 4, :].bitcast(I32),
            )
        load_w(0)
        load_w(1)
        nc.sync.dma_start(offs2_sb[:], offs2)
        nc.sync.dma_start(wgo_sb[:, 0:LEAD], wgo[:, 0:LEAD])
        load_w(2)
        nc.sync.dma_start(wgo_sb[:, LEAD:S], wgo[:, LEAD:S])
        load_w(3)

        nc.vector.transpose(wgt_turned[:], wgt_cut[:])
        halves = [slice(0, S // 2), slice(S // 2, S)]
        for u, cols in enumerate(halves):
            nc.vector.tensor_copy(
                wgt_wide[:, cols].rearrange("p (s h r) -> p s h r", h=2, r=GROUP),
                wgt_turned[:]
                .rearrange("p (h u s) -> p u s h", h=2, u=2)[:, u]
                .unsqueeze(3)
                .to_broadcast([P, GROUP // 2, 2, GROUP]),
            )
        nc.gpsimd.memset(windows[1][:].bitcast(I32), 0)
        for cols in halves:
            nc.vector.transpose(wgt_sb[:, cols], wgt_wide[:, cols])

        b_psum = psum_b.tile([P, P], F32, name="b_psum")
        nc.tensor.transpose(b_psum[:], b_rows[:], ident[:])
        nc.scalar.copy(out=b_col[:], in_=b_psum[:, 0:ROW_TILES])
        nc.scalar.copy(out=b_held[:], in_=b_psum[:, AHEAD - 1 : AHEAD])

        def gather(dst, a, i, first, end):
            nc.vector.tensor_tensor(
                dst,
                x_sb[a][i][:].indirect(offs_sb[:, first // 16 : end // 16]),
                wgt_sb[:, first:end],
                MULT,
            )

        def interleave(dst, planes):
            nc.scalar.copy(
                out=dst.rearrange("p (c i t) -> p c t i", i=4, t=PACK),
                in_=planes.rearrange("p t (c i) -> p c t i", i=4),
            )

        def quantize_last(first, end, src):
            nc.vector.quantize_mx(out=codes2[:, first:end].bitcast(FP8X4), scales=scales2[:, first:end], in_=src)

        def project(r, cuts):
            acc = psum.tile([P, S], F32, name="acc")
            n = max(n for n in range(len(W_CUTS) - 1) if W_CUTS[n] <= r)
            w_first = (r - W_CUTS[n]) * P
            steps = [(a, cuts[c], cuts[c + 1]) for a in range(PASSES) for c in range(len(cuts) - 1)]
            for step, (a, first, end) in enumerate(steps):
                nc.tensor.matmul_mx(
                    out=acc[:, first:end],
                    lhsT=w_sb[n][:, a, w_first : w_first + P].bitcast(FP8X4),
                    lhsT_scale=w_scale[4 * a :, r * P : (r + 1) * P],
                    rhs=codes[a][:, first:end].bitcast(FP8X4),
                    rhs_scale=scales[a][:, first:end],
                    start=(step == 0),
                    stop=(step == len(steps) - 1),
                )
            first, end = cuts[0], cuts[-1]
            bias = b_held[:] if (r, first) == (AHEAD - 1, 0) else b_col[:, r : r + 1]
            nc.scalar.activation(acted_cols(r, first, end), acc[:, first:end], GELU, bias=bias)

        def scatter(r, first, end):
            nc.vector.tensor_tensor(
                windows[r % WINDOWS][:].indirect(offs2_sb[:, first // 16 : end // 16]),
                acted_cols(r, first, end),
                wgo_sb[:, first:end],
                MULT,
            )

        def store(r):
            rows = out[r * P : (r + 1) * P, :]
            window = windows[r % WINDOWS]
            nc.sync.dma_start(rows[:, 0 : T // 2], window[:, 0 : T // 2])
            second = nc.scalar if r == ROW_TILES - 1 else nc.sync
            second.dma_start(rows[:, T // 2 : T], window[:, T // 2 : T])

        for a in range(LAST):
            for i in range(PACK):
                gather(picked[a][:, i, :], a, i, 0, S)
                if (a, i) == (0, 0):
                    nc.gpsimd.memset(windows[2][:].bitcast(I32), 0)
            interleave(grouped01[:, a * S * PACK : (a + 1) * S * PACK], picked[a][:])
        for i in range(2):
            gather(last[:, i * S : (i + 1) * S], LAST, i, 0, S)
        for i in range(2):
            gather(last_lead[:, 1, i, :], LAST, 2 + i, 0, LEAD)
        nc.scalar.copy(
            out=grouped_lead[:].rearrange("p (c i u v) -> p c u v i", i=4, u=2, v=2),
            in_=last_lead.rearrange("p u v (c i) -> p c u v i", i=4),
        )
        nc.vector.quantize_mx(out=codes01[:].bitcast(FP8X4), scales=scales01[:], in_=grouped01[:])
        quantize_last(0, LEAD, grouped_lead[:])
        for r in range(AHEAD):
            project(r, (0, LEAD))
        for i in (2, 3):
            gather(last_rest[:, i, :], LAST, i, LEAD, S)
            nc.gpsimd.memset(windows[AHEAD + i - 2][:].bitcast(I32), 0)
        interleave(grouped_rest[:], last_rest)
        for r in range(AHEAD):
            scatter(r, 0, LEAD)
        for r in range(AHEAD, EARLY):
            project(r, (0, LEAD))
        quantize_last(LEAD, S - LEAD, grouped_rest[:, 0 : (REST - LEAD) * PACK])
        quantize_last(S - LEAD, S, grouped_rest[:, (REST - LEAD) * PACK : REST * PACK])
        for r in range(AHEAD, EARLY):
            scatter(r, 0, LEAD)
        for r in range(EARLY):
            project(r, (LEAD, S - LEAD, S))
            scatter(r, LEAD, S)
            store(r)
        for r in range(EARLY, ROW_TILES):
            project(r, (0, S))
            scatter(r, 0, S)
            store(r)
